import numpy as np
import ml_dtypes


def mxq(x, axis, fmt="e4m3"):
    dtype, down = {"e4m3": (ml_dtypes.float8_e4m3fn, 7), "e5m2": (ml_dtypes.float8_e5m2, 14)}[fmt]
    v = np.moveaxis(np.asarray(x, np.float32).astype(ml_dtypes.bfloat16).astype(np.float64), axis, -1)
    blocks = v.reshape(v.shape[:-1] + (-1, 32))
    amax = np.abs(blocks).max(-1, keepdims=True)
    byte = np.maximum(np.where(amax > 0, np.frexp(amax)[1] - 1 + 127, 0) - down, 1)
    scale = np.exp2(byte - 127.0)
    codes = (blocks / scale).astype(np.float32).astype(dtype).astype(np.float64)
    return np.moveaxis((codes * scale).reshape(v.shape), -1, axis)


WIDE = False


def mx_kscale(k):
    if not WIDE:
        return np.ones(k)
    levels = np.array([10, -10, 5, -5, 0])
    if k % 512:
        return np.exp2(np.random.permutation(np.resize(levels, k // 32))).repeat(32)
    a = np.empty((k // 512, 16))
    for p in range(k // 512):
        a[p, :8] = np.random.permutation(np.resize(levels, 8))
        for g in range(8):
            far = levels[np.abs(levels - a[p, g]) >= 10]
            a[p, g + 8] = far[np.random.randint(len(far))]
    return np.exp2(a.ravel()).repeat(32)


def f64(x):
    return np.asarray(x).astype(np.float64)


def striped(idx):
    return np.tile(np.asarray(idx).reshape(-1, 16).T, (8, 1)).astype(np.uint16)


def unstriped(offs):
    return offs[:16].T.reshape(-1).astype(np.int64)


E2M1 = np.array([0.0, 0.5, 1.0, 1.5, 2.0, 3.0, 4.0, 6.0, -0.0, -0.5, -1.0, -1.5, -2.0, -3.0, -4.0, -6.0])


def pack_weight(w, fmt):
    k, n = w.shape
    w = f64(np.asarray(w, np.float32).astype(ml_dtypes.bfloat16)).reshape(k // 32, 32, n)
    amax = np.abs(w).max(1)
    if fmt == "e4m3":
        byte = np.frexp(amax)[1] - 1 + 127 - 7
    else:
        mant, ex = np.frexp(amax / 6.0)
        byte = np.where(mant > 0.5, ex, ex - 1) + 127
    byte = np.clip(np.where(amax > 0, byte, 1), 1, 254)
    scaled = (w * np.exp2(127.0 - byte)[:, None, :]).reshape(k, n).astype(np.float32)
    by_word = np.ascontiguousarray(scaled.reshape(k // 512, 128, 4, n).transpose(0, 1, 3, 2))
    if fmt == "e4m3":
        words = by_word.astype(ml_dtypes.float8_e4m3fn).view(np.uint8)
    else:
        c = by_word.astype(ml_dtypes.float4_e2m1fn).view(np.uint8) & 0xF
        words = (c[..., 0::2] | (c[..., 1::2] << 4)).reshape(k // 512, 128, 2 * n)
    return np.ascontiguousarray(words), np.ascontiguousarray(byte.astype(np.uint8).reshape(k // 512, 16, n))


def unpack_weight(words, scales, fmt):
    g, _, n = scales.shape
    words = np.ascontiguousarray(words).reshape(g, 128, n, -1)
    if fmt == "e4m3":
        vals = words.view(ml_dtypes.float8_e4m3fn).astype(np.float64)
    else:
        nib = np.empty((g, 128, n, 4), np.uint8)
        nib[..., 0::2] = words & 0xF
        nib[..., 1::2] = words >> 4
        vals = E2M1[nib]
    vals = vals * np.repeat(np.exp2(scales.astype(np.float64) - 127.0), 8, axis=1)[..., None]
    return vals.transpose(0, 1, 3, 2).reshape(g * 512, n)


D, T, I, Q, E, U = 512, 2048, 512, 128, 512, 512


def setup_inputs():
    n = np.random.standard_normal
    idx = np.random.permutation(T)[:I]
    idx2 = np.random.randint(0, U, I)
    fd = mx_kscale(D)
    fi = mx_kscale(I)
    ti = np.ones(T)
    ti[idx] = fi
    remp = pack_weight(n((D, T)) * 0.7 / fd[:, None], "e4m3")
    return {
        "query": (n((D, Q)) * 0.25 / np.sqrt(D) * fd[:, None]).astype(np.float32),
        "cent": (n((D, U)) / fd[:, None]).astype(np.float32),
        "rem_words": remp[0],
        "rem_scales": remp[1],
        "size": (np.random.uniform(0.5, 2.0, (1, I)) * fi).astype(np.float32),
        "vals": (n((E, T)) / ti).astype(np.float32),
        "offs": striped(idx),
        "offs2": striped(idx2),
    }


def reference(query, cent, rem_words, rem_scales, size, vals, offs, offs2):
    idx = unstriped(offs)
    idx2 = unstriped(offs2)
    remu = unpack_weight(rem_words, rem_scales, "e4m3")
    queryq = mxq(f64(query), 0, "e4m3")
    centq = mxq(f64(cent), 0, "e4m3")
    c1 = queryq.T @ centq
    remidxg = remu[:, idx]
    b = queryq.T @ remidxg
    s = c1[:, idx2] + b
    p = np.exp(s - np.max(s, axis=1, keepdims=True))
    w = p * f64(size) / np.sum(p, axis=1, keepdims=True)
    wt = w.T
    vt = f64(vals)[:, idx].T
    wtq = mxq(wt, 0, "e4m3")
    vtq = mxq(vt, 0, "e4m3")
    o = wtq.T @ vtq
    return o

@@ -1,0 +1,182 @@
+from contextlib import ExitStack
+
+import concourse.mybir as mybir
+from concourse.masks import make_identity
+
+D, T, I, Q, E, U = 512, 2048, 512, 128, 512, 512
+FLOPS = 2 * Q * (D * U + D * I + I * E)
+
+F32 = mybir.dt.float32
+BF16 = mybir.dt.bfloat16
+I32 = mybir.dt.int32
+U32 = mybir.dt.uint32
+U16 = mybir.dt.uint16
+U8 = mybir.dt.uint8
+FP8X4 = mybir.dt.float8_e4m3fn_x4
+ALU = mybir.AluOpType
+ACT = mybir.ActivationFunctionType
+AXIS = mybir.AxisListType
+
+P = 128
+PACK = 4
+SPARE = 192
+BLOCKS = E // P
+
+
+def interleave(copy, grouped, raw):
+    copy(out=grouped.rearrange("p (c i) t -> p c t i", i=4), in_=raw.rearrange("p t (c i) -> p c t i", i=4))
+
+
+def tile_attend_centreremainder_kernel(tc, query, cent, rem_words, rem_scales, size, vals, offs, offs2, out):
+    nc = tc.nc
+    with ExitStack() as ctx:
+        keep = ctx.enter_context(tc.tile_pool(name="keep", bufs=1))
+        psum = ctx.enter_context(tc.psum_pool(name="psum", bufs=1))
+        turn = ctx.enter_context(tc.psum_pool(name="turn", bufs=2))
+
+        def sbuf(name, shape, dtype, slot=None):
+            return keep.tile(shape, dtype, name=name, tag=slot or name, align_bytes=64)
+
+        def quantise(name, grouped, width, slot=None):
+            codes = sbuf(name + "_codes", [P, width], U32, slot)
+            scales = sbuf(name + "_scales", [P, width], U8)
+            nc.vector.quantize_mx(out=codes[:].bitcast(FP8X4), scales=scales[:], in_=grouped)
+            return codes, scales
+
+        def columns(operand, first, width):
+            return operand[0][:, first : first + width].bitcast(FP8X4), operand[1][:, first : first + width]
+
+        def product(acc, stationary, moving):
+            nc.tensor.matmul_mx(
+                out=acc,
+                lhsT=stationary[0],
+                lhsT_scale=stationary[1],
+                rhs=moving[0],
+                rhs_scale=moving[1],
+                start=True,
+                stop=True,
+            )
+
+        scale_pool = sbuf("scale_pool", [P, T], U8)
+        nc.vector.memset(scale_pool[:].bitcast(I32), 0)
+        c1 = sbuf("c1", [P, U + SPARE], F32)
+        nc.vector.memset(c1[:, U:], 0.0)
+        warm_out = sbuf("warm_out", [P, 1], F32)
+        nc.scalar.activation(out=warm_out[:], in_=c1[:, U : U + 1], func=ACT.Exp)
+        identity = sbuf("identity", [P, P], F32)
+        make_identity(nc, identity[:])
+
+        token_list = keep.tile([P, I // 16], U16, name="token_list")
+        nc.sync.dma_start(token_list[:], offs)
+        centre_list = keep.tile([P, I // 16], U16, name="centre_list")
+        nc.sync.dma_start(centre_list[:], offs2)
+        query_raw = sbuf("query_raw", [P, PACK, Q], F32)
+        nc.scalar.dma_start(out=query_raw[:], in_=query.rearrange("(p t) q -> p t q", t=PACK))
+        cent_chunks = ((0, 256, nc.vector.tensor_copy), (256, 128, nc.scalar.copy), (384, 128, nc.vector.tensor_copy))
+        cent_raw = []
+        for n, (first, width, copy) in enumerate(cent_chunks):
+            raw = sbuf("cent_raw%d" % n, [P, PACK, width], F32)
+            nc.sync.dma_start(out=raw[:], in_=cent[:, first : first + width].rearrange("(p t) u -> p t u", t=PACK))
+            cent_raw.append(raw)
+        size_cols = sbuf("size_cols", [P, PACK], F32)
+        nc.gpsimd.dma_start(out=size_cols[:], in_=size.rearrange("o (p t) -> (o p) t", t=PACK))
+        for quad in range(4):
+            nc.sync.dma_start(
+                out=scale_pool[32 * quad : 32 * quad + 4, :].bitcast(I32),
+                in_=rem_scales[0, 4 * quad : 4 * quad + 4, :].bitcast(I32),
+            )
+        word_pool = sbuf("word_pool", [P, T], I32, "words")
+        nc.sync.dma_start(out=word_pool[:], in_=rem_words[0].rearrange("p n t -> p (n t)").bitcast(I32))
+        val_pool = []
+        for blk in range(BLOCKS):
+            pool_rows = sbuf("val_pool%d" % blk, [P, T], F32, "val%d" % blk)
+            nc.sync.dma_start(out=pool_rows[:], in_=vals[blk * P : (blk + 1) * P, :])
+            val_pool.append(pool_rows)
+
+        query_grouped = sbuf("query_grouped", [P, Q, PACK], BF16)
+        interleave(nc.vector.tensor_copy, query_grouped[:], query_raw[:])
+        query_mx = columns(quantise("query", query_grouped[:].rearrange("p q t -> p (q t)"), Q), 0, Q)
+
+        cent_grouped = []
+        for n, (first, width, copy) in enumerate(cent_chunks):
+            grouped = sbuf("cent_grouped%d" % n, [P, width, PACK], BF16, "cent%d" % n)
+            interleave(copy, grouped[:], cent_raw[n][:])
+            cent_grouped.append(grouped)
+        c1_banks = [psum.tile([P, U // 2], F32, name="c1_bank%d" % h, tag="c1_bank%d" % h) for h in range(2)]
+        for n, (first, width, copy) in enumerate(cent_chunks):
+            cent_mx = quantise("cent%d" % n, cent_grouped[n][:].rearrange("p u t -> p (u t)"), width)
+            h, at = divmod(first, U // 2)
+            product(c1_banks[h][:, at : at + width], query_mx, columns(cent_mx, 0, width))
+        for h in range(2):
+            nc.scalar.copy(out=c1[:, h * (U // 2) : (h + 1) * (U // 2)], in_=c1_banks[h][:])
+
+        rem_bytes = sbuf("rem_bytes", [P, I], U8, "cent1")
+        nc.vector.tensor_copy(rem_bytes[:], scale_pool[:].indirect(token_list[:]))
+        rem_codes = sbuf("rem_codes", [P, I], U32, "cent2")
+        nc.vector.tensor_copy(rem_codes[:], word_pool[:].bitcast(U32).indirect(token_list[:]))
+        b_bank = psum.tile([P, I], F32, name="b_bank")
+        product(b_bank[:], query_mx, columns((rem_codes, rem_bytes), 0, I))
+        c1_picked = sbuf("c1_picked", [P, I], F32, "words")
+        nc.vector.tensor_copy(c1_picked[:], c1[:].indirect(centre_list[:]))
+
+        size_bank = psum.tile([P, PACK, P], F32, name="size_bank", tag="c1_bank0")
+        for t in range(PACK):
+            nc.tensor.transpose(size_bank[:, t, :], size_cols[:, t : t + 1].to_broadcast([P, P]), identity[:])
+
+        def turn_slots(rows, grouped):
+            words = rows[:].bitcast(F32)
+            bank = turn.tile([P, 2, P], F32, name="turn_bank")
+            for u in range(2):
+                nc.tensor.transpose(bank[:, u, :], words[:, u : 2 * P : 2], identity[:])
+            nc.scalar.copy(
+                out=grouped.bitcast(F32).rearrange("p (r u) -> p r u", u=2),
+                in_=bank[:].rearrange("p u r -> p r u"),
+            )
+
+        def gather_values(blk, slot, grouped):
+            picked = sbuf("picked%d" % blk, [P, I], BF16, slot)
+            nc.vector.tensor_copy(picked[:], val_pool[blk][:].indirect(token_list[:]))
+            turn_slots(picked, grouped)
+
+        early = sbuf("early_grouped", [P, BLOCKS * I], BF16)
+        last = sbuf("last_grouped", [P, I], BF16)
+
+        s = sbuf("s", [P, I], F32)
+        nc.vector.tensor_tensor(s[:], c1_picked[:], b_bank[:], ALU.add)
+        neg_max = sbuf("neg_max", [P, 1], F32)
+        nc.vector.tensor_reduce(out=neg_max[:], in_=s[:], axis=AXIS.X, op=ALU.max, negate=True)
+        p = sbuf("p", [P, I], F32, "p")
+        row_sum = sbuf("row_sum", [P, 1], F32, "row_sum")
+        nc.scalar.activation(out=p[:], in_=s[:], func=ACT.Exp, bias=neg_max[:], scale=1.0, accum_out=row_sum[:])
+        gather_values(0, "words", early[:, I : 2 * I])
+        inv_sum = sbuf("inv_sum", [P, 1], F32, "val0")
+        nc.vector.reciprocal(out=inv_sum[:], in_=row_sum[:])
+        w = sbuf("w", [P, I], BF16)
+        nc.vector.scalar_tensor_tensor(
+            out=w[:].rearrange("p (n t) -> p n t", t=PACK),
+            in0=p[:].rearrange("p (n t) -> p n t", t=PACK),
+            scalar=inv_sum[:],
+            in1=size_bank[:].rearrange("p t n -> p n t"),
+            op0=ALU.mult,
+            op1=ALU.mult,
+        )
+
+        turn_slots(w, early[:, :I])
+        gather_values(1, "row_sum", early[:, 2 * I : 3 * I])
+        gather_values(2, "p", early[:, 3 * I :])
+        gather_values(3, "val1", last[:])
+        early_mx = quantise("early", early[:], BLOCKS * P, "val3")
+        last_mx = quantise("last", last[:], P)
+        w_mx = columns(early_mx, 0, P)
+
+        head_bank = psum.tile([P, 3 * P], F32, name="head_bank")
+        product(head_bank[:, : 2 * P], w_mx, columns(early_mx, P, 2 * P))
+        product(head_bank[:, 2 * P :], w_mx, columns(early_mx, 3 * P, P))
+        head = sbuf("head", [P, 3 * P], F32)
+        nc.scalar.copy(out=head[:], in_=head_bank[:])
+        nc.sync.dma_start(out=out[:, : 3 * P], in_=head[:])
+        tail_bank = psum.tile([P, P], F32, name="tail_bank")
+        product(tail_bank[:], w_mx, columns(last_mx, 0, P))
+        tail = sbuf("tail", [P, P], F32)
+        nc.scalar.copy(out=tail[:], in_=tail_bank[:])
+        nc.sync.dma_start(out=out[:, 3 * P :], in_=tail[:])

@@ -21,6 +21,7 @@ P = 128
 PACK = 4
 SPARE = 192
 BLOCKS = E // P
+VECTOR_SHARE = 352
 
 
 def interleave(copy, grouped, raw):
@@ -66,20 +67,14 @@ def tile_attend_centreremainder_kernel(tc, query, cent, rem_words, rem_scales, s
         identity = sbuf("identity", [P, P], F32)
         make_identity(nc, identity[:])
 
-        token_list = keep.tile([P, I // 16], U16, name="token_list")
-        nc.sync.dma_start(token_list[:], offs)
         centre_list = keep.tile([P, I // 16], U16, name="centre_list")
         nc.sync.dma_start(centre_list[:], offs2)
+        cent_raw = sbuf("cent_raw", [P, PACK, U], F32)
+        nc.sync.dma_start(out=cent_raw[:], in_=cent.rearrange("(p t) u -> p t u", t=PACK))
         query_raw = sbuf("query_raw", [P, PACK, Q], F32)
-        nc.scalar.dma_start(out=query_raw[:], in_=query.rearrange("(p t) q -> p t q", t=PACK))
-        cent_chunks = ((0, 256, nc.vector.tensor_copy), (256, 128, nc.scalar.copy), (384, 128, nc.vector.tensor_copy))
-        cent_raw = []
-        for n, (first, width, copy) in enumerate(cent_chunks):
-            raw = sbuf("cent_raw%d" % n, [P, PACK, width], F32)
-            nc.sync.dma_start(out=raw[:], in_=cent[:, first : first + width].rearrange("(p t) u -> p t u", t=PACK))
-            cent_raw.append(raw)
-        size_cols = sbuf("size_cols", [P, PACK], F32)
-        nc.gpsimd.dma_start(out=size_cols[:], in_=size.rearrange("o (p t) -> (o p) t", t=PACK))
+        nc.sync.dma_start(out=query_raw[:], in_=query.rearrange("(p t) q -> p t q", t=PACK))
+        token_list = keep.tile([P, I // 16], U16, name="token_list")
+        nc.sync.dma_start(token_list[:], offs)
         for quad in range(4):
             nc.sync.dma_start(
                 out=scale_pool[32 * quad : 32 * quad + 4, :].bitcast(I32),
@@ -87,26 +82,29 @@ def tile_attend_centreremainder_kernel(tc, query, cent, rem_words, rem_scales, s
             )
         word_pool = sbuf("word_pool", [P, T], I32, "words")
         nc.sync.dma_start(out=word_pool[:], in_=rem_words[0].rearrange("p n t -> p (n t)").bitcast(I32))
-        val_pool = []
-        for blk in range(BLOCKS):
+        size_cols = sbuf("size_cols", [P, PACK], F32)
+        nc.sync.dma_start(out=size_cols[:], in_=size.rearrange("o (p t) -> (o p) t", t=PACK))
+        val_halves = []
+        for h in range(2):
+            half = sbuf("val_half%d" % h, [P, T // 2], F32)
+            nc.sync.dma_start(out=half[:], in_=vals[:P, h * (T // 2) : (h + 1) * (T // 2)])
+            val_halves.append(half)
+        val_pool = {}
+        for blk in range(1, BLOCKS):
             pool_rows = sbuf("val_pool%d" % blk, [P, T], F32, "val%d" % blk)
             nc.sync.dma_start(out=pool_rows[:], in_=vals[blk * P : (blk + 1) * P, :])
-            val_pool.append(pool_rows)
+            val_pool[blk] = pool_rows
 
-        query_grouped = sbuf("query_grouped", [P, Q, PACK], BF16)
-        interleave(nc.vector.tensor_copy, query_grouped[:], query_raw[:])
+        cent_grouped = sbuf("cent_grouped", [P, U, PACK], BF16, "cent1")
+        interleave(nc.vector.tensor_copy, cent_grouped[:, :VECTOR_SHARE, :], cent_raw[:, :, :VECTOR_SHARE])
+        interleave(nc.scalar.copy, cent_grouped[:, VECTOR_SHARE:, :], cent_raw[:, :, VECTOR_SHARE:])
+        cent_mx = quantise("cent", cent_grouped[:].rearrange("p u t -> p (u t)"), U)
+        query_grouped = sbuf("query_grouped", [P, Q, PACK], BF16, "cent2")
+        interleave(nc.scalar.copy, query_grouped[:], query_raw[:])
         query_mx = columns(quantise("query", query_grouped[:].rearrange("p q t -> p (q t)"), Q), 0, Q)
-
-        cent_grouped = []
-        for n, (first, width, copy) in enumerate(cent_chunks):
-            grouped = sbuf("cent_grouped%d" % n, [P, width, PACK], BF16, "cent%d" % n)
-            interleave(copy, grouped[:], cent_raw[n][:])
-            cent_grouped.append(grouped)
         c1_banks = [psum.tile([P, U // 2], F32, name="c1_bank%d" % h, tag="c1_bank%d" % h) for h in range(2)]
-        for n, (first, width, copy) in enumerate(cent_chunks):
-            cent_mx = quantise("cent%d" % n, cent_grouped[n][:].rearrange("p u t -> p (u t)"), width)
-            h, at = divmod(first, U // 2)
-            product(c1_banks[h][:, at : at + width], query_mx, columns(cent_mx, 0, width))
+        for h in range(2):
+            product(c1_banks[h][:], query_mx, columns(cent_mx, h * (U // 2), U // 2))
         for h in range(2):
             nc.scalar.copy(out=c1[:, h * (U // 2) : (h + 1) * (U // 2)], in_=c1_banks[h][:])
 
@@ -141,6 +139,14 @@ def tile_attend_centreremainder_kernel(tc, query, cent, rem_words, rem_scales, s
         early = sbuf("early_grouped", [P, BLOCKS * I], BF16)
         last = sbuf("last_grouped", [P, I], BF16)
 
+        val_rounded = sbuf("val_rounded", [P, T], BF16, "p")
+        for h in range(2):
+            nc.scalar.activation(
+                out=val_rounded[:, h * (T // 2) : (h + 1) * (T // 2)], in_=val_halves[h][:], func=ACT.Copy
+            )
+        picked0 = sbuf("picked0", [P, I], BF16)
+        nc.scalar.activation(out=picked0[:], in_=val_rounded[:].indirect(token_list[:]), func=ACT.Copy)
+
         s = sbuf("s", [P, I], F32)
         nc.vector.tensor_tensor(s[:], c1_picked[:], b_bank[:], ALU.add)
         neg_max = sbuf("neg_max", [P, 1], F32)
@@ -148,8 +154,9 @@ def tile_attend_centreremainder_kernel(tc, query, cent, rem_words, rem_scales, s
         p = sbuf("p", [P, I], F32, "p")
         row_sum = sbuf("row_sum", [P, 1], F32, "row_sum")
         nc.scalar.activation(out=p[:], in_=s[:], func=ACT.Exp, bias=neg_max[:], scale=1.0, accum_out=row_sum[:])
-        gather_values(0, "words", early[:, I : 2 * I])
-        inv_sum = sbuf("inv_sum", [P, 1], F32, "val0")
+        turn_slots(picked0, early[:, I : 2 * I])
+        gather_values(1, "words", early[:, 2 * I : 3 * I])
+        inv_sum = sbuf("inv_sum", [P, 1], F32, "val1")
         nc.vector.reciprocal(out=inv_sum[:], in_=row_sum[:])
         w = sbuf("w", [P, I], BF16)
         nc.vector.scalar_tensor_tensor(
@@ -162,9 +169,8 @@ def tile_attend_centreremainder_kernel(tc, query, cent, rem_words, rem_scales, s
         )
 
         turn_slots(w, early[:, :I])
-        gather_values(1, "row_sum", early[:, 2 * I : 3 * I])
-        gather_values(2, "p", early[:, 3 * I :])
-        gather_values(3, "val1", last[:])
+        gather_values(2, "row_sum", early[:, 3 * I :])
+        gather_values(3, "p", last[:])
         early_mx = quantise("early", early[:], BLOCKS * P, "val3")
         last_mx = quantise("last", last[:], P)
         w_mx = columns(early_mx, 0, P)

@@ -28,6 +28,10 @@ def interleave(copy, grouped, raw):
     copy(out=grouped.rearrange("p (c i) t -> p c t i", i=4), in_=raw.rearrange("p t (c i) -> p c t i", i=4))
 
 
+def dealt(tile):
+    return tile[:].rearrange("p (u g j) -> p g u j", u=2, j=16)
+
+
 def tile_attend_centreremainder_kernel(tc, query, cent, rem_words, rem_scales, size, vals, offs, offs2, out):
     nc = tc.nc
     with ExitStack() as ctx:
@@ -75,10 +79,10 @@ def tile_attend_centreremainder_kernel(tc, query, cent, rem_words, rem_scales, s
         nc.sync.dma_start(out=query_raw[:], in_=query.rearrange("(p t) q -> p t q", t=PACK))
         token_list = keep.tile([P, I // 16], U16, name="token_list")
         nc.sync.dma_start(token_list[:], offs)
-        for quad in range(4):
+        for row in range(4):
             nc.sync.dma_start(
-                out=scale_pool[32 * quad : 32 * quad + 4, :].bitcast(I32),
-                in_=rem_scales[0, 4 * quad : 4 * quad + 4, :].bitcast(I32),
+                out=scale_pool[row:P:32, :].bitcast(I32),
+                in_=rem_scales[0, row:16:4, :].bitcast(I32),
             )
         word_pool = sbuf("word_pool", [P, T], I32, "words")
         nc.sync.dma_start(out=word_pool[:], in_=rem_words[0].rearrange("p n t -> p (n t)").bitcast(I32))
@@ -86,7 +90,7 @@ def tile_attend_centreremainder_kernel(tc, query, cent, rem_words, rem_scales, s
         nc.sync.dma_start(out=size_cols[:], in_=size.rearrange("o (p t) -> (o p) t", t=PACK))
         val_halves = []
         for h in range(2):
-            half = sbuf("val_half%d" % h, [P, T // 2], F32)
+            half = sbuf("val_half%d" % h, [P, T // 2], F32, "half%d" % h)
             nc.sync.dma_start(out=half[:], in_=vals[:P, h * (T // 2) : (h + 1) * (T // 2)])
             val_halves.append(half)
         val_pool = {}
@@ -125,7 +129,7 @@ def tile_attend_centreremainder_kernel(tc, query, cent, rem_words, rem_scales, s
             words = rows[:].bitcast(F32)
             bank = turn.tile([P, 2, P], F32, name="turn_bank")
             for u in range(2):
-                nc.tensor.transpose(bank[:, u, :], words[:, u : 2 * P : 2], identity[:])
+                nc.tensor.transpose(bank[:, u, :], words[:, u * P : (u + 1) * P], identity[:])
             nc.scalar.copy(
                 out=grouped.bitcast(F32).rearrange("p (r u) -> p r u", u=2),
                 in_=bank[:].rearrange("p u r -> p r u"),
@@ -133,44 +137,45 @@ def tile_attend_centreremainder_kernel(tc, query, cent, rem_words, rem_scales, s
 
         def gather_values(blk, slot, grouped):
             picked = sbuf("picked%d" % blk, [P, I], BF16, slot)
-            nc.vector.tensor_copy(picked[:], val_pool[blk][:].indirect(token_list[:]))
+            nc.vector.tensor_copy(dealt(picked), val_pool[blk][:].indirect(token_list[:]))
             turn_slots(picked, grouped)
 
         early = sbuf("early_grouped", [P, BLOCKS * I], BF16)
         last = sbuf("last_grouped", [P, I], BF16)
 
-        val_rounded = sbuf("val_rounded", [P, T], BF16, "p")
+        val_rounded = sbuf("val_rounded", [P, T], BF16)
         for h in range(2):
             nc.scalar.activation(
                 out=val_rounded[:, h * (T // 2) : (h + 1) * (T // 2)], in_=val_halves[h][:], func=ACT.Copy
             )
-        picked0 = sbuf("picked0", [P, I], BF16)
-        nc.scalar.activation(out=picked0[:], in_=val_rounded[:].indirect(token_list[:]), func=ACT.Copy)
 
-        s = sbuf("s", [P, I], F32)
+        s = sbuf("s", [P, I], F32, "s")
         nc.vector.tensor_tensor(s[:], c1_picked[:], b_bank[:], ALU.add)
         neg_max = sbuf("neg_max", [P, 1], F32)
         nc.vector.tensor_reduce(out=neg_max[:], in_=s[:], axis=AXIS.X, op=ALU.max, negate=True)
-        p = sbuf("p", [P, I], F32, "p")
+        p = sbuf("p", [P, I], F32, "half1")
         row_sum = sbuf("row_sum", [P, 1], F32, "row_sum")
         nc.scalar.activation(out=p[:], in_=s[:], func=ACT.Exp, bias=neg_max[:], scale=1.0, accum_out=row_sum[:])
+        picked0 = sbuf("picked0", [P, I], BF16, "s")
+        nc.scalar.activation(out=dealt(picked0), in_=val_rounded[:].indirect(token_list[:]), func=ACT.Copy)
         turn_slots(picked0, early[:, I : 2 * I])
         gather_values(1, "words", early[:, 2 * I : 3 * I])
-        inv_sum = sbuf("inv_sum", [P, 1], F32, "val1")
-        nc.vector.reciprocal(out=inv_sum[:], in_=row_sum[:])
-        w = sbuf("w", [P, I], BF16)
-        nc.vector.scalar_tensor_tensor(
-            out=w[:].rearrange("p (n t) -> p n t", t=PACK),
-            in0=p[:].rearrange("p (n t) -> p n t", t=PACK),
-            scalar=inv_sum[:],
-            in1=size_bank[:].rearrange("p t n -> p n t"),
-            op0=ALU.mult,
-            op1=ALU.mult,
+        weighted = sbuf("weighted", [P, I + 1], F32, "val1")
+        sized, inv_sum = weighted[:, :I], weighted[:, I:]
+        nc.vector.reciprocal(out=inv_sum, in_=row_sum[:])
+        nc.vector.tensor_tensor(
+            sized.rearrange("p (n t) -> p n t", t=PACK),
+            p[:].rearrange("p (n t) -> p n t", t=PACK),
+            size_bank[:].rearrange("p t n -> p n t"),
+            ALU.mult,
         )
-
+        w = sbuf("w", [P, I], BF16)
+        nc.scalar.activation(
+            out=dealt(w), in_=sized.rearrange("p (g u j) -> p g u j", u=2, j=16), func=ACT.Copy, scale=inv_sum
+        )
         turn_slots(w, early[:, :I])
         gather_values(2, "row_sum", early[:, 3 * I :])
-        gather_values(3, "p", last[:])
+        gather_values(3, "half1", last[:])
         early_mx = quantise("early", early[:], BLOCKS * P, "val3")
         last_mx = quantise("last", last[:], P)
         w_mx = columns(early_mx, 0, P)
@@ -184,5 +189,5 @@ def tile_attend_centreremainder_kernel(tc, query, cent, rem_words, rem_scales, s
         tail_bank = psum.tile([P, P], F32, name="tail_bank")
         product(tail_bank[:], w_mx, columns(last_mx, 0, P))
         tail = sbuf("tail", [P, P], F32)
-        nc.scalar.copy(out=tail[:], in_=tail_bank[:])
+        nc.vector.tensor_copy(out=tail[:], in_=tail_bank[:])
         nc.sync.dma_start(out=out[:, 3 * P :], in_=tail[:])

@@ -19,6 +19,9 @@ AXIS = mybir.AxisListType
 
 P = 128
 PACK = 4
+LIST_ROWS = 16
+SCALE_ROWS = D // 32
+QUADRANT = 32
 SPARE = 192
 BLOCKS = E // P
 VECTOR_SHARE = 352
@@ -39,11 +42,11 @@ def tile_attend_centreremainder_kernel(tc, query, cent, rem_words, rem_scales, s
         psum = ctx.enter_context(tc.psum_pool(name="psum", bufs=1))
         turn = ctx.enter_context(tc.psum_pool(name="turn", bufs=2))
 
-        def sbuf(name, shape, dtype, slot=None):
-            return keep.tile(shape, dtype, name=name, tag=slot or name, align_bytes=64)
+        def sbuf(name, shape, dtype, reuses=None):
+            return keep.tile(shape, dtype, name=name, tag=reuses or name, align_bytes=64)
 
-        def quantise(name, grouped, width, slot=None):
-            codes = sbuf(name + "_codes", [P, width], U32, slot)
+        def quantise(name, grouped, width, reuses=None):
+            codes = sbuf(name + "_codes", [P, width], U32, reuses)
             scales = sbuf(name + "_scales", [P, width], U8)
             nc.vector.quantize_mx(out=codes[:].bitcast(FP8X4), scales=scales[:], in_=grouped)
             return codes, scales
@@ -66,44 +69,42 @@ def tile_attend_centreremainder_kernel(tc, query, cent, rem_words, rem_scales, s
         nc.vector.memset(scale_pool[:].bitcast(I32), 0)
         c1 = sbuf("c1", [P, U + SPARE], F32)
         nc.vector.memset(c1[:, U:], 0.0)
-        warm_out = sbuf("warm_out", [P, 1], F32)
-        nc.scalar.activation(out=warm_out[:], in_=c1[:, U : U + 1], func=ACT.Exp)
         identity = sbuf("identity", [P, P], F32)
         make_identity(nc, identity[:])
 
-        centre_list = keep.tile([P, I // 16], U16, name="centre_list")
-        nc.sync.dma_start(centre_list[:], offs2)
         cent_raw = sbuf("cent_raw", [P, PACK, U], F32)
         nc.sync.dma_start(out=cent_raw[:], in_=cent.rearrange("(p t) u -> p t u", t=PACK))
         query_raw = sbuf("query_raw", [P, PACK, Q], F32)
         nc.sync.dma_start(out=query_raw[:], in_=query.rearrange("(p t) q -> p t q", t=PACK))
-        token_list = keep.tile([P, I // 16], U16, name="token_list")
+        token_list = keep.tile([P, I // LIST_ROWS], U16, name="token_list")
         nc.sync.dma_start(token_list[:], offs)
         for row in range(4):
             nc.sync.dma_start(
-                out=scale_pool[row:P:32, :].bitcast(I32),
-                in_=rem_scales[0, row:16:4, :].bitcast(I32),
+                out=scale_pool[row:P:QUADRANT, :].bitcast(I32),
+                in_=rem_scales[0, row:SCALE_ROWS:4, :].bitcast(I32),
             )
-        word_pool = sbuf("word_pool", [P, T], I32, "words")
+        word_pool = sbuf("word_pool", [P, T], I32)
         nc.sync.dma_start(out=word_pool[:], in_=rem_words[0].rearrange("p n t -> p (n t)").bitcast(I32))
+        centre_list = keep.tile([P, I // LIST_ROWS], U16, name="centre_list")
+        nc.sync.dma_start(centre_list[:], offs2)
         size_cols = sbuf("size_cols", [P, PACK], F32)
         nc.sync.dma_start(out=size_cols[:], in_=size.rearrange("o (p t) -> (o p) t", t=PACK))
         val_halves = []
         for h in range(2):
-            half = sbuf("val_half%d" % h, [P, T // 2], F32, "half%d" % h)
+            half = sbuf("val_half%d" % h, [P, T // 2], F32)
             nc.sync.dma_start(out=half[:], in_=vals[:P, h * (T // 2) : (h + 1) * (T // 2)])
             val_halves.append(half)
         val_pool = {}
         for blk in range(1, BLOCKS):
-            pool_rows = sbuf("val_pool%d" % blk, [P, T], F32, "val%d" % blk)
+            pool_rows = sbuf("val_pool%d" % blk, [P, T], F32)
             nc.sync.dma_start(out=pool_rows[:], in_=vals[blk * P : (blk + 1) * P, :])
             val_pool[blk] = pool_rows
 
-        cent_grouped = sbuf("cent_grouped", [P, U, PACK], BF16, "cent1")
+        cent_grouped = sbuf("cent_grouped", [P, U, PACK], BF16)
         interleave(nc.vector.tensor_copy, cent_grouped[:, :VECTOR_SHARE, :], cent_raw[:, :, :VECTOR_SHARE])
         interleave(nc.scalar.copy, cent_grouped[:, VECTOR_SHARE:, :], cent_raw[:, :, VECTOR_SHARE:])
         cent_mx = quantise("cent", cent_grouped[:].rearrange("p u t -> p (u t)"), U)
-        query_grouped = sbuf("query_grouped", [P, Q, PACK], BF16, "cent2")
+        query_grouped = sbuf("query_grouped", [P, Q, PACK], BF16)
         interleave(nc.scalar.copy, query_grouped[:], query_raw[:])
         query_mx = columns(quantise("query", query_grouped[:].rearrange("p q t -> p (q t)"), Q), 0, Q)
         c1_banks = [psum.tile([P, U // 2], F32, name="c1_bank%d" % h, tag="c1_bank%d" % h) for h in range(2)]
@@ -112,13 +113,13 @@ def tile_attend_centreremainder_kernel(tc, query, cent, rem_words, rem_scales, s
         for h in range(2):
             nc.scalar.copy(out=c1[:, h * (U // 2) : (h + 1) * (U // 2)], in_=c1_banks[h][:])
 
-        rem_bytes = sbuf("rem_bytes", [P, I], U8, "cent1")
+        rem_bytes = sbuf("rem_bytes", [P, I], U8, reuses="cent_grouped")
         nc.vector.tensor_copy(rem_bytes[:], scale_pool[:].indirect(token_list[:]))
-        rem_codes = sbuf("rem_codes", [P, I], U32, "cent2")
+        rem_codes = sbuf("rem_codes", [P, I], U32, reuses="query_grouped")
         nc.vector.tensor_copy(rem_codes[:], word_pool[:].bitcast(U32).indirect(token_list[:]))
         b_bank = psum.tile([P, I], F32, name="b_bank")
         product(b_bank[:], query_mx, columns((rem_codes, rem_bytes), 0, I))
-        c1_picked = sbuf("c1_picked", [P, I], F32, "words")
+        c1_picked = sbuf("c1_picked", [P, I], F32, reuses="word_pool")
         nc.vector.tensor_copy(c1_picked[:], c1[:].indirect(centre_list[:]))
 
         size_bank = psum.tile([P, PACK, P], F32, name="size_bank", tag="c1_bank0")
@@ -135,12 +136,13 @@ def tile_attend_centreremainder_kernel(tc, query, cent, rem_words, rem_scales, s
                 in_=bank[:].rearrange("p u r -> p r u"),
             )
 
-        def gather_values(blk, slot, grouped):
-            picked = sbuf("picked%d" % blk, [P, I], BF16, slot)
+        def gather_values(blk, reuses, grouped):
+            picked = sbuf("picked%d" % blk, [P, I], BF16, reuses)
             nc.vector.tensor_copy(dealt(picked), val_pool[blk][:].indirect(token_list[:]))
             turn_slots(picked, grouped)
 
-        early = sbuf("early_grouped", [P, BLOCKS * I], BF16)
+        early = sbuf("early_grouped", [P, 2 * I], BF16)
+        middle = sbuf("middle_grouped", [P, 2 * I], BF16)
         last = sbuf("last_grouped", [P, I], BF16)
 
         val_rounded = sbuf("val_rounded", [P, T], BF16)
@@ -148,19 +150,19 @@ def tile_attend_centreremainder_kernel(tc, query, cent, rem_words, rem_scales, s
             nc.scalar.activation(
                 out=val_rounded[:, h * (T // 2) : (h + 1) * (T // 2)], in_=val_halves[h][:], func=ACT.Copy
             )
+        picked0 = sbuf("picked0", [P, I], BF16)
+        nc.scalar.activation(out=dealt(picked0), in_=val_rounded[:].indirect(token_list[:]), func=ACT.Copy)
 
-        s = sbuf("s", [P, I], F32, "s")
+        s = sbuf("s", [P, I], F32)
         nc.vector.tensor_tensor(s[:], c1_picked[:], b_bank[:], ALU.add)
         neg_max = sbuf("neg_max", [P, 1], F32)
         nc.vector.tensor_reduce(out=neg_max[:], in_=s[:], axis=AXIS.X, op=ALU.max, negate=True)
-        p = sbuf("p", [P, I], F32, "half1")
-        row_sum = sbuf("row_sum", [P, 1], F32, "row_sum")
+        p = sbuf("p", [P, I], F32, reuses="val_rounded")
+        row_sum = sbuf("row_sum", [P, 1], F32)
         nc.scalar.activation(out=p[:], in_=s[:], func=ACT.Exp, bias=neg_max[:], scale=1.0, accum_out=row_sum[:])
-        picked0 = sbuf("picked0", [P, I], BF16, "s")
-        nc.scalar.activation(out=dealt(picked0), in_=val_rounded[:].indirect(token_list[:]), func=ACT.Copy)
-        turn_slots(picked0, early[:, I : 2 * I])
-        gather_values(1, "words", early[:, 2 * I : 3 * I])
-        weighted = sbuf("weighted", [P, I + 1], F32, "val1")
+        turn_slots(picked0, early[:, :I])
+        gather_values(1, "word_pool", early[:, I:])
+        weighted = sbuf("weighted", [P, I + 1], F32, reuses="val_pool1")
         sized, inv_sum = weighted[:, :I], weighted[:, I:]
         nc.vector.reciprocal(out=inv_sum, in_=row_sum[:])
         nc.vector.tensor_tensor(
@@ -173,16 +175,18 @@ def tile_attend_centreremainder_kernel(tc, query, cent, rem_words, rem_scales, s
         nc.scalar.activation(
             out=dealt(w), in_=sized.rearrange("p (g u j) -> p g u j", u=2, j=16), func=ACT.Copy, scale=inv_sum
         )
-        turn_slots(w, early[:, :I])
-        gather_values(2, "row_sum", early[:, 3 * I :])
-        gather_values(3, "half1", last[:])
-        early_mx = quantise("early", early[:], BLOCKS * P, "val3")
+        turn_slots(w, middle[:, :I])
+
+        gather_values(2, "row_sum", middle[:, I:])
+        early_mx = quantise("early", early[:], 2 * P, reuses="val_pool2")
+        gather_values(3, "val_rounded", last[:])
+        middle_mx = quantise("middle", middle[:], 2 * P, reuses="val_pool3")
         last_mx = quantise("last", last[:], P)
-        w_mx = columns(early_mx, 0, P)
+        w_mx = columns(middle_mx, 0, P)
 
         head_bank = psum.tile([P, 3 * P], F32, name="head_bank")
-        product(head_bank[:, : 2 * P], w_mx, columns(early_mx, P, 2 * P))
-        product(head_bank[:, 2 * P :], w_mx, columns(early_mx, 3 * P, P))
+        product(head_bank[:, : 2 * P], w_mx, columns(early_mx, 0, 2 * P))
+        product(head_bank[:, 2 * P :], w_mx, columns(middle_mx, P, P))
         head = sbuf("head", [P, 3 * P], F32)
         nc.scalar.copy(out=head[:], in_=head_bank[:])
         nc.sync.dma_start(out=out[:, : 3 * P], in_=head[:])

from contextlib import ExitStack

import concourse.mybir as mybir
from concourse.masks import make_identity

D, T, I, Q, E, U = 512, 2048, 512, 128, 512, 512
FLOPS = 2 * Q * (D * U + D * I + I * E)

F32 = mybir.dt.float32
BF16 = mybir.dt.bfloat16
I32 = mybir.dt.int32
U32 = mybir.dt.uint32
U16 = mybir.dt.uint16
U8 = mybir.dt.uint8
FP8X4 = mybir.dt.float8_e4m3fn_x4
ALU = mybir.AluOpType
ACT = mybir.ActivationFunctionType
AXIS = mybir.AxisListType

P = 128
PACK = 4
LIST_ROWS = 16
SCALE_ROWS = D // 32
QUADRANT = 32
SPARE = 192
BLOCKS = E // P
VECTOR_SHARE = 352


def interleave(copy, grouped, raw):
    copy(out=grouped.rearrange("p (c i) t -> p c t i", i=4), in_=raw.rearrange("p t (c i) -> p c t i", i=4))


def dealt(tile):
    return tile[:].rearrange("p (u g j) -> p g u j", u=2, j=16)


def tile_attend_centreremainder_kernel(tc, query, cent, rem_words, rem_scales, size, vals, offs, offs2, out):
    nc = tc.nc
    with ExitStack() as ctx:
        keep = ctx.enter_context(tc.tile_pool(name="keep", bufs=1))
        psum = ctx.enter_context(tc.psum_pool(name="psum", bufs=1))
        turn = ctx.enter_context(tc.psum_pool(name="turn", bufs=2))

        def sbuf(name, shape, dtype, reuses=None):
            return keep.tile(shape, dtype, name=name, tag=reuses or name, align_bytes=64)

        def quantise(name, grouped, width, reuses=None):
            codes = sbuf(name + "_codes", [P, width], U32, reuses)
            scales = sbuf(name + "_scales", [P, width], U8)
            nc.vector.quantize_mx(out=codes[:].bitcast(FP8X4), scales=scales[:], in_=grouped)
            return codes, scales

        def columns(operand, first, width):
            return operand[0][:, first : first + width].bitcast(FP8X4), operand[1][:, first : first + width]

        def product(acc, stationary, moving):
            nc.tensor.matmul_mx(
                out=acc,
                lhsT=stationary[0],
                lhsT_scale=stationary[1],
                rhs=moving[0],
                rhs_scale=moving[1],
                start=True,
                stop=True,
            )

        scale_pool = sbuf("scale_pool", [P, T], U8)
        nc.vector.memset(scale_pool[:].bitcast(I32), 0)
        c1 = sbuf("c1", [P, U + SPARE], F32)
        nc.vector.memset(c1[:, U:], 0.0)
        identity = sbuf("identity", [P, P], F32)
        make_identity(nc, identity[:])

        cent_raw = sbuf("cent_raw", [P, PACK, U], F32)
        nc.sync.dma_start(out=cent_raw[:], in_=cent.rearrange("(p t) u -> p t u", t=PACK))
        query_raw = sbuf("query_raw", [P, PACK, Q], F32)
        nc.sync.dma_start(out=query_raw[:], in_=query.rearrange("(p t) q -> p t q", t=PACK))
        token_list = keep.tile([P, I // LIST_ROWS], U16, name="token_list")
        nc.sync.dma_start(token_list[:], offs)
        for row in range(4):
            nc.sync.dma_start(
                out=scale_pool[row:P:QUADRANT, :].bitcast(I32),
                in_=rem_scales[0, row:SCALE_ROWS:4, :].bitcast(I32),
            )
        word_pool = sbuf("word_pool", [P, T], I32)
        nc.sync.dma_start(out=word_pool[:], in_=rem_words[0].rearrange("p n t -> p (n t)").bitcast(I32))
        centre_list = keep.tile([P, I // LIST_ROWS], U16, name="centre_list")
        nc.sync.dma_start(centre_list[:], offs2)
        size_cols = sbuf("size_cols", [P, PACK], F32)
        nc.sync.dma_start(out=size_cols[:], in_=size.rearrange("o (p t) -> (o p) t", t=PACK))
        val_halves = []
        for h in range(2):
            half = sbuf("val_half%d" % h, [P, T // 2], F32)
            nc.sync.dma_start(out=half[:], in_=vals[:P, h * (T // 2) : (h + 1) * (T // 2)])
            val_halves.append(half)
        val_pool = {}
        for blk in range(1, BLOCKS):
            pool_rows = sbuf("val_pool%d" % blk, [P, T], F32)
            nc.sync.dma_start(out=pool_rows[:], in_=vals[blk * P : (blk + 1) * P, :])
            val_pool[blk] = pool_rows

        cent_grouped = sbuf("cent_grouped", [P, U, PACK], BF16)
        interleave(nc.vector.tensor_copy, cent_grouped[:, :VECTOR_SHARE, :], cent_raw[:, :, :VECTOR_SHARE])
        interleave(nc.scalar.copy, cent_grouped[:, VECTOR_SHARE:, :], cent_raw[:, :, VECTOR_SHARE:])
        cent_mx = quantise("cent", cent_grouped[:].rearrange("p u t -> p (u t)"), U)
        query_grouped = sbuf("query_grouped", [P, Q, PACK], BF16)
        interleave(nc.scalar.copy, query_grouped[:], query_raw[:])
        query_mx = columns(quantise("query", query_grouped[:].rearrange("p q t -> p (q t)"), Q), 0, Q)
        c1_banks = [psum.tile([P, U // 2], F32, name="c1_bank%d" % h, tag="c1_bank%d" % h) for h in range(2)]
        for h in range(2):
            product(c1_banks[h][:], query_mx, columns(cent_mx, h * (U // 2), U // 2))
        for h in range(2):
            nc.scalar.copy(out=c1[:, h * (U // 2) : (h + 1) * (U // 2)], in_=c1_banks[h][:])

        rem_bytes = sbuf("rem_bytes", [P, I], U8, reuses="cent_grouped")
        nc.vector.tensor_copy(rem_bytes[:], scale_pool[:].indirect(token_list[:]))
        rem_codes = sbuf("rem_codes", [P, I], U32, reuses="query_grouped")
        nc.vector.tensor_copy(rem_codes[:], word_pool[:].bitcast(U32).indirect(token_list[:]))
        b_bank = psum.tile([P, I], F32, name="b_bank")
        product(b_bank[:], query_mx, columns((rem_codes, rem_bytes), 0, I))
        c1_picked = sbuf("c1_picked", [P, I], F32, reuses="word_pool")
        nc.vector.tensor_copy(c1_picked[:], c1[:].indirect(centre_list[:]))

        size_bank = psum.tile([P, PACK, P], F32, name="size_bank", tag="c1_bank0")
        for t in range(PACK):
            nc.tensor.transpose(size_bank[:, t, :], size_cols[:, t : t + 1].to_broadcast([P, P]), identity[:])

        def turn_slots(rows, grouped):
            words = rows[:].bitcast(F32)
            bank = turn.tile([P, 2, P], F32, name="turn_bank")
            for u in range(2):
                nc.tensor.transpose(bank[:, u, :], words[:, u * P : (u + 1) * P], identity[:])
            nc.scalar.copy(
                out=grouped.bitcast(F32).rearrange("p (r u) -> p r u", u=2),
                in_=bank[:].rearrange("p u r -> p r u"),
            )

        def gather_values(blk, reuses, grouped):
            picked = sbuf("picked%d" % blk, [P, I], BF16, reuses)
            nc.vector.tensor_copy(dealt(picked), val_pool[blk][:].indirect(token_list[:]))
            turn_slots(picked, grouped)

        early = sbuf("early_grouped", [P, 2 * I], BF16)
        middle = sbuf("middle_grouped", [P, 2 * I], BF16)
        last = sbuf("last_grouped", [P, I], BF16)

        val_rounded = sbuf("val_rounded", [P, T], BF16)
        for h in range(2):
            nc.scalar.activation(
                out=val_rounded[:, h * (T // 2) : (h + 1) * (T // 2)], in_=val_halves[h][:], func=ACT.Copy
            )
        picked0 = sbuf("picked0", [P, I], BF16)
        nc.scalar.activation(out=dealt(picked0), in_=val_rounded[:].indirect(token_list[:]), func=ACT.Copy)

        s = sbuf("s", [P, I], F32)
        nc.vector.tensor_tensor(s[:], c1_picked[:], b_bank[:], ALU.add)
        neg_max = sbuf("neg_max", [P, 1], F32)
        nc.vector.tensor_reduce(out=neg_max[:], in_=s[:], axis=AXIS.X, op=ALU.max, negate=True)
        p = sbuf("p", [P, I], F32, reuses="val_rounded")
        row_sum = sbuf("row_sum", [P, 1], F32)
        nc.scalar.activation(out=p[:], in_=s[:], func=ACT.Exp, bias=neg_max[:], scale=1.0, accum_out=row_sum[:])
        turn_slots(picked0, early[:, :I])
        gather_values(1, "word_pool", early[:, I:])
        weighted = sbuf("weighted", [P, I + 1], F32, reuses="val_pool1")
        sized, inv_sum = weighted[:, :I], weighted[:, I:]
        nc.vector.reciprocal(out=inv_sum, in_=row_sum[:])
        nc.vector.tensor_tensor(
            sized.rearrange("p (n t) -> p n t", t=PACK),
            p[:].rearrange("p (n t) -> p n t", t=PACK),
            size_bank[:].rearrange("p t n -> p n t"),
            ALU.mult,
        )
        w = sbuf("w", [P, I], BF16)
        nc.scalar.activation(
            out=dealt(w), in_=sized.rearrange("p (g u j) -> p g u j", u=2, j=16), func=ACT.Copy, scale=inv_sum
        )
        turn_slots(w, middle[:, :I])

        gather_values(2, "row_sum", middle[:, I:])
        early_mx = quantise("early", early[:], 2 * P, reuses="val_pool2")
        gather_values(3, "val_rounded", last[:])
        middle_mx = quantise("middle", middle[:], 2 * P, reuses="val_pool3")
        last_mx = quantise("last", last[:], P)
        w_mx = columns(middle_mx, 0, P)

        head_bank = psum.tile([P, 3 * P], F32, name="head_bank")
        product(head_bank[:, : 2 * P], w_mx, columns(early_mx, 0, 2 * P))
        product(head_bank[:, 2 * P :], w_mx, columns(middle_mx, P, P))
        head = sbuf("head", [P, 3 * P], F32)
        nc.scalar.copy(out=head[:], in_=head_bank[:])
        nc.sync.dma_start(out=out[:, : 3 * P], in_=head[:])
        tail_bank = psum.tile([P, P], F32, name="tail_bank")
        product(tail_bank[:], w_mx, columns(last_mx, 0, P))
        tail = sbuf("tail", [P, P], F32)
        nc.vector.tensor_copy(out=tail[:], in_=tail_bank[:])
        nc.sync.dma_start(out=out[:, 3 * P :], in_=tail[:])
